import numpy as np
import ml_dtypes


def mxq(x, axis, fmt="e4m3"):
    dtype, down = {"e4m3": (ml_dtypes.float8_e4m3fn, 7), "e5m2": (ml_dtypes.float8_e5m2, 14)}[fmt]
    v = np.moveaxis(np.asarray(x, np.float32).astype(ml_dtypes.bfloat16).astype(np.float64), axis, -1)
    blocks = v.reshape(v.shape[:-1] + (-1, 32))
    amax = np.abs(blocks).max(-1, keepdims=True)
    byte = np.maximum(np.where(amax > 0, np.frexp(amax)[1] - 1 + 127, 0) - down, 1)
    scale = np.exp2(byte - 127.0)
    codes = (blocks / scale).astype(np.float32).astype(dtype).astype(np.float64)
    return np.moveaxis((codes * scale).reshape(v.shape), -1, axis)


WIDE = False


def mx_kscale(k):
    if not WIDE:
        return np.ones(k)
    levels = np.array([10, -10, 5, -5, 0])
    if k % 512:
        return np.exp2(np.random.permutation(np.resize(levels, k // 32))).repeat(32)
    a = np.empty((k // 512, 16))
    for p in range(k // 512):
        a[p, :8] = np.random.permutation(np.resize(levels, 8))
        for g in range(8):
            far = levels[np.abs(levels - a[p, g]) >= 10]
            a[p, g + 8] = far[np.random.randint(len(far))]
    return np.exp2(a.ravel()).repeat(32)


def f64(x):
    return np.asarray(x).astype(np.float64)


def striped(idx):
    return np.tile(idx.reshape(-1, 16).T, (8, 1)).astype(np.uint16)


def unstriped(offs):
    return offs[:16].T.reshape(-1).astype(np.int64)


def striped8(idx):
    return np.concatenate([x.reshape(-1, 16).T for x in idx]).astype(np.uint16)


def runs(offs, k):
    lists = np.stack([offs[16 * r : 16 * r + 16].T.reshape(-1) for r in range(8)]).astype(np.int64)
    return lists[np.arange(k) % 512 // 64]


def pack_weight(w):
    k, n = w.shape
    w = f64(np.asarray(w, np.float32).astype(ml_dtypes.bfloat16)).reshape(k // 32, 32, n)
    amax = np.abs(w).max(1)
    byte = np.clip(np.where(amax > 0, np.frexp(amax)[1] - 1 + 127 - 7, 1), 1, 254)
    scaled = (w * np.exp2(127.0 - byte)[:, None, :]).reshape(k, n).astype(np.float32)
    words = np.ascontiguousarray(scaled.reshape(k // 512, 128, 4, n).transpose(0, 1, 3, 2)).astype(ml_dtypes.float8_e4m3fn).view(np.uint8)
    return words, np.ascontiguousarray(byte.astype(np.uint8).reshape(k // 512, 16, n))


def unpack_weight(words, scales):
    g, p, n, _ = words.shape
    vals = np.ascontiguousarray(words).view(ml_dtypes.float8_e4m3fn).astype(np.float64) * np.repeat(np.exp2(scales.astype(np.float64) - 127.0), 8, axis=1)[..., None]
    return vals.transpose(0, 1, 3, 2).reshape(g * 512, n)

def planes(y):
    n, m = y.shape
    v = y.astype(np.float32).astype(ml_dtypes.bfloat16).astype(np.float64).reshape(n // 32, 32, m)
    top = np.abs(v).max(1)
    byte = np.clip(np.where(top > 0, np.frexp(top)[1] - 1 + 127 - 7, 1), 1, 254)
    codes = (v * np.exp2(127.0 - byte)[:, None, :]).reshape(n, m).astype(np.float32).astype(ml_dtypes.float8_e4m3fn).view(np.uint8)
    words = codes.reshape(n // 512, 128, 4, m).transpose(0, 1, 3, 2)
    return np.ascontiguousarray(words), np.ascontiguousarray(byte.astype(np.uint8).reshape(n // 512, 16, m))


K, T, S, G, H, W, C = 512, 1024, 256, 2048, 512, 128, 512


def setup_inputs():
    n = np.random.standard_normal
    s = mx_kscale(K)[:, None]
    packed_xT = pack_weight(n((K, T)) * s)
    packed_dT = pack_weight(n((K, G)) / s)
    perm = np.random.permutation(S)
    return {
        "x_words": packed_xT[0],
        "x_scales": packed_xT[1],
        "d_words": packed_dT[0],
        "d_scales": packed_dT[1],
        "gs": (np.random.uniform(0.5, 1.5, (K, 1)) / s).astype(np.float32),
        "offs": striped8(np.random.randint(0, T, (8, S))),
        "k1": striped8(np.random.randint(0, G, (8, H))),
        "n1": striped(perm[:W]),
        "n2": striped(perm[W:]),
        "n3": striped(np.random.permutation(S)),
        "cand": striped8(np.random.randint(0, T, (8, C))),
        "n4": striped(np.random.permutation(S)),
        "n5": striped(np.random.permutation(S)),
    }


def reference(x_words, x_scales, d_words, d_scales, gs, offs, k1, n1, n2, n3, cand, n4, n5):
    x_cand = unpack_weight(x_words, x_scales)[np.arange(K)[:, None], runs(cand, K)]
    d_k1 = unpack_weight(d_words, d_scales)[np.arange(K)[:, None], runs(k1, K)]
    xq = unpack_weight(x_words, x_scales)[np.arange(K)[:, None], runs(offs, K)]
    h = 0.0625 * (d_k1.T @ xq)
    pa = h[:, unstriped(n1)]
    pb = h[:, unstriped(n2)]
    rb = pa - pb
    ra = pa + pb
    ds = np.zeros((H, S))
    ds[:, unstriped(n1)] = ra
    dt = ds.copy()
    dt[:, unstriped(n2)] = rb
    z = f64(gs) * (np.maximum(dt, dt[:, unstriped(n3)]))
    s = 0.0625 * ((x_cand.T @ mxq(z, 0, "e4m3")))
    ds2 = np.zeros((C, S))
    ds2[:, unstriped(n4)] = s
    ds3 = np.zeros((C, S))
    ds3[:, unstriped(n5)] = s
    out_0 = np.maximum(ds2, ds3)
    return (out_0,) + planes(out_0)

@@ -1,0 +1,249 @@
+from contextlib import ExitStack
+
+import concourse.mybir as mybir
+
+K, T, S, G, H, W, C = 512, 1024, 256, 2048, 512, 128, 512
+FLOPS = 2 * K * H * S + 2 * H * C * S
+
+F32 = mybir.dt.float32
+BF16 = mybir.dt.bfloat16
+I32 = mybir.dt.int32
+U32 = mybir.dt.uint32
+U16 = mybir.dt.uint16
+U8 = mybir.dt.uint8
+FP8X4 = mybir.dt.float8_e4m3fn_x4
+ALU = mybir.AluOpType
+COPY = mybir.ActivationFunctionType.Copy
+
+P = 128
+PACK = 4
+HALF = S // 2
+SIXTEENTH = 0.0625
+
+
+def tile_picked_hpqhhaarhsendtwo_none_po_kernel(
+    tc, x_words, x_scales, d_words, d_scales, gs, offs, k1, n1, n2, n3, cand, n4, n5, out_0, out_1, out_2
+):
+    nc = tc.nc
+
+    with ExitStack() as ctx:
+        lists = ctx.enter_context(tc.tile_pool(name="lists", bufs=1))
+        sb = ctx.enter_context(tc.tile_pool(name="sb", bufs=1))
+        psum = ctx.enter_context(tc.psum_pool(name="psum", bufs=8))
+
+        def load_list(source, name):
+            tile = lists.tile(list(source.shape), U16, name=name)
+            nc.sync.dma_start(tile[:], source)
+            return tile
+
+        def load_scale_rows(source, name):
+            tile = sb.tile([P, source.shape[2]], U8, name=name, align_bytes=64)
+            nc.vector.memset(tile[:].bitcast(I32), 0)
+            for e in range(2):
+                nc.sync.dma_start(tile[e:P:16, :].bitcast(I32), source[0, e:16:2, :].bitcast(I32))
+            return tile
+
+        def load_words(source, name):
+            tile = sb.tile([P, source.shape[2]], U32, name=name, align_bytes=64)
+            nc.sync.dma_start(tile[:].bitcast(I32), source[0].rearrange("p c r -> p (c r)").bitcast(I32))
+            return tile
+
+        def pick(out, table, offsets, pieces):
+            n = out.shape[1] // pieces
+            for i in range(pieces):
+                nc.vector.tensor_copy(
+                    out[:, i * n : (i + 1) * n], table[:].indirect(offsets[:, i * n // 16 : (i + 1) * n // 16])
+                )
+
+        def deal_words(out, picked):
+            nc.vector.tensor_copy(
+                out.rearrange("p (t c i) -> p c t i", t=PACK, i=4),
+                picked.rearrange("p (c i t) -> p c t i", t=PACK, i=4),
+            )
+
+        def deal_bytes(out, picked):
+            nc.vector.tensor_copy(
+                out.rearrange("p (t m) -> p t m", t=PACK), picked.rearrange("p (m t) -> p t m", t=PACK)
+            )
+
+        def lift_odd_runs(plane):
+            for e in range(2):
+                nc.sync.dma_start(plane[2 + e : P : 32, :].bitcast(I32), plane[16 + e : P : 32, :].bitcast(I32))
+
+        k1_t = load_list(k1, "k1_t")
+        d_bytes = load_scale_rows(d_scales, "d_bytes")
+        offs_t = load_list(offs, "offs_t")
+        x_bytes = load_scale_rows(x_scales, "x_bytes")
+        n1_t = load_list(n1, "n1_t")
+        d_table = load_words(d_words, "d_table")
+        x_table = load_words(x_words, "x_table")
+        n2_t = load_list(n2, "n2_t")
+        cand_t = load_list(cand, "cand_t")
+        n3_t = load_list(n3, "n3_t")
+        n4_t = load_list(n4, "n4_t")
+        n5_t = load_list(n5, "n5_t")
+        gs_t = sb.tile([P, PACK], F32, name="gs_t")
+        nc.gpsimd.dma_start(gs_t[:], gs.rearrange("(p t) o -> p (t o)", t=PACK))
+        gain = sb.tile([P, PACK], F32, name="gain")
+        nc.scalar.activation(gain[:], gs_t[:], COPY, scale=SIXTEENTH)
+
+        dk_bytes = sb.tile([P, H], U8, name="dk_bytes", tag="bytes_a", align_bytes=64)
+        xq_bytes = sb.tile([P, S], U8, name="xq_bytes", align_bytes=64)
+        plane1 = sb.tile([P, H + S], U8, name="plane1", tag="bytes_b", align_bytes=64)
+        pick(dk_bytes, d_bytes, k1_t, 1)
+        pick(xq_bytes, x_bytes, offs_t, 1)
+        deal_bytes(plane1[:, :H], dk_bytes[:])
+        nc.vector.tensor_copy(plane1[:, H:].bitcast(I32), xq_bytes[:].bitcast(I32))
+        lift_odd_runs(plane1)
+
+        dk_words = sb.tile([P, H], U32, name="dk_words", tag="words_a", align_bytes=64)
+        dk_dealt = sb.tile([P, H], U32, name="dk_dealt", tag="words_b", align_bytes=64)
+        xq_words = sb.tile([P, S], U32, name="xq_words", align_bytes=64)
+        pick(dk_words, d_table, k1_t, 1)
+        deal_words(dk_dealt[:], dk_words[:])
+        pick(xq_words, x_table, offs_t, 1)
+
+        h = []
+        for t in range(PACK):
+            rows = slice(t * P, (t + 1) * P)
+            acc = psum.tile([P, S], F32, name="acc", tag="acc")
+            nc.tensor.matmul_mx(
+                out=acc[:],
+                lhsT=dk_dealt[:, rows].bitcast(FP8X4),
+                lhsT_scale=plane1[:, rows],
+                rhs=xq_words[:].bitcast(FP8X4),
+                rhs_scale=plane1[:, H:],
+                start=True,
+                stop=True,
+            )
+            h_t = sb.tile([P, S], F32, name=f"h{t}")
+            nc.vector.tensor_copy(h_t[:], acc[:])
+            h.append(h_t)
+
+        pair = [sb.tile([P, S], F32, name=f"pair{t}") for t in range(PACK)]
+        mixed = [sb.tile([P, S], F32, name=f"mixed{t}", tag=f"mixed{t}") for t in range(PACK)]
+        dt = [sb.tile([P, S], F32, name=f"dt{t}") for t in range(PACK)]
+        other_a = sb.tile([P, PACK, HALF], F32, name="other_a")
+        top = sb.tile([P, PACK, S], F32, name="top")
+        z_bf = [sb.tile([P, HALF, PACK], BF16, name=f"z_bf{c}", align_bytes=64) for c in range(2)]
+        z_words = sb.tile([P, S], U32, name="z_words", align_bytes=64)
+        z_plane = sb.tile([P, S], U8, name="z_plane", align_bytes=64)
+
+        def fetch_pair(t, side):
+            offsets = (n1_t, n2_t)[side]
+            nc.scalar.activation(pair[t][:, side * W : (side + 1) * W], h[t][:].indirect(offsets[:]), COPY)
+
+        def mix(t):
+            pa, pb = pair[t][:, :W], pair[t][:, W:]
+            nc.vector.tensor_tensor(mixed[t][:, :W], pa, pb, ALU.add)
+            nc.vector.tensor_tensor(mixed[t][:, W:], pa, pb, ALU.subtract)
+
+        def put_pair(t, side):
+            offsets = (n1_t, n2_t)[side]
+            nc.scalar.activation(dt[t][:].indirect(offsets[:]), mixed[t][:, side * W : (side + 1) * W], COPY)
+
+        def fetch_other(t, c, other):
+            offsets = n3_t[:, c * HALF // 16 : (c + 1) * HALF // 16]
+            nc.scalar.activation(other[:, t, :], dt[t][:].indirect(offsets), COPY)
+
+        def weigh(t, c, other):
+            cols = slice(c * HALF, (c + 1) * HALF)
+            nc.vector.tensor_tensor(top[:, t, cols], dt[t][:, cols], other[:, t, :], ALU.max)
+            nc.vector.tensor_scalar(z_bf[c][:, :, t], top[:, t, cols], gain[:, t : t + 1], None, ALU.mult)
+
+        def quantise_z(c):
+            cols = slice(c * HALF, (c + 1) * HALF)
+            nc.vector.quantize_mx(
+                out=z_words[:, cols].bitcast(FP8X4),
+                scales=z_plane[:, cols],
+                in_=z_bf[c][:].rearrange("p w j -> p (w j)"),
+            )
+
+        for t in range(2):
+            fetch_pair(t, 0)
+            fetch_pair(t, 1)
+            mix(t)
+        for t in range(PACK):
+            for side in range(2):
+                put_pair(t, side)
+                if t + 2 < PACK:
+                    fetch_pair(t + 2, side)
+                else:
+                    step = 2 * (t + 2 - PACK) + side
+                    fetch_other(step, 0, other_a)
+                    weigh(step, 0, other_a)
+            if t + 2 < PACK:
+                mix(t + 2)
+
+        xc_bytes = sb.tile([P, C], U8, name="xc_bytes", tag="bytes_b", align_bytes=64)
+        plane2 = sb.tile([P, C], U8, name="plane2", tag="bytes_a", align_bytes=64)
+        xc_words = sb.tile([P, C], U32, name="xc_words", tag="words_b", align_bytes=64)
+        xc_dealt = sb.tile([P, C], U32, name="xc_dealt", tag="words_a", align_bytes=64)
+        pick(xc_bytes, x_bytes, cand_t, 2)
+        deal_bytes(plane2[:], xc_bytes[:])
+        lift_odd_runs(plane2)
+        pick(xc_words, x_table, cand_t, 2)
+        deal_words(xc_dealt[:], xc_words[:])
+
+        s = [sb.tile([P, S], F32, name=f"s{t}") for t in range(PACK)]
+
+        def score(t, cols):
+            rows = slice(t * P, (t + 1) * P)
+            acc = psum.tile([P, cols.stop - cols.start], F32, name="acc", tag="acc")
+            nc.tensor.matmul_mx(
+                out=acc[:],
+                lhsT=xc_dealt[:, rows].bitcast(FP8X4),
+                lhsT_scale=plane2[:, rows],
+                rhs=z_words[:, cols].bitcast(FP8X4),
+                rhs_scale=z_plane[:, cols],
+                start=True,
+                stop=True,
+            )
+            nc.vector.tensor_scalar(s[t][:, cols], acc[:], SIXTEENTH, None, ALU.mult)
+
+        quantise_z(0)
+        score(0, slice(0, HALF))
+
+        other_b = sb.tile([P, PACK, HALF], F32, name="other_b", tag=f"mixed{PACK - 1}")
+        for t in range(PACK):
+            fetch_other(t, 1, other_b)
+            weigh(t, 1, other_b)
+        quantise_z(1)
+        score(0, slice(HALF, S))
+        for t in range(1, PACK):
+            score(t, slice(0, S))
+
+        y_bf = [sb.tile([P, HALF, PACK], BF16, name=f"y_bf{c}", align_bytes=64) for c in range(2)]
+        y_words = sb.tile([P, S], U32, name="y_words", align_bytes=64)
+        y_plane = sb.tile([P, S], U8, name="y_plane", align_bytes=64)
+        out_rows = out_0.rearrange("(p t) c -> p t c", t=PACK)
+        for t in range(PACK):
+            ds2 = sb.tile([P, 2 * S], F32, name=f"ds2_{t}")
+            ds3 = sb.tile([P, 2 * S], F32, name=f"ds3_{t}")
+            pieces = 2 if t == 0 else 1
+            n = S // pieces
+            for i in range(pieces):
+                for window, offsets in ((ds2, n4_t), (ds3, n5_t)):
+                    nc.scalar.activation(
+                        window[:].indirect(offsets[:, i * n // 16 : (i + 1) * n // 16]),
+                        s[t][:, i * n : (i + 1) * n],
+                        COPY,
+                    )
+            y = sb.tile([P, S], F32, name=f"y{t}")
+            for c in range(2):
+                cols = slice(c * HALF, (c + 1) * HALF)
+                nc.vector.tensor_tensor(y[:, cols], ds2[:, cols], ds3[:, cols], ALU.max)
+            nc.sync.dma_start(out_rows[:, t, :], y[:])
+            for c in range(2):
+                nc.vector.tensor_copy(y_bf[c][:, :, t], y[:, c * HALF : (c + 1) * HALF])
+        for c in range(2):
+            cols = slice(c * HALF, (c + 1) * HALF)
+            nc.vector.quantize_mx(
+                out=y_words[:, cols].bitcast(FP8X4),
+                scales=y_plane[:, cols],
+                in_=y_bf[c][:].rearrange("p w j -> p (w j)"),
+            )
+        nc.sync.dma_start(out_1[0].rearrange("p c r -> p (c r)").bitcast(I32), y_words[:].bitcast(I32))
+        for q in range(4):
+            queue = (nc.scalar, nc.sync)[q % 2]
+            queue.dma_start(out_2[0, 4 * q : 4 * q + 4, :].bitcast(I32), y_plane[32 * q : 32 * q + 4, :].bitcast(I32))

@@ -18,6 +18,8 @@ COPY = mybir.ActivationFunctionType.Copy
 P = 128
 PACK = 4
 HALF = S // 2
+EARLY = 64
+LATE = S - EARLY
 SIXTEENTH = 0.0625
 
 
@@ -39,8 +41,7 @@ def tile_picked_hpqhhaarhsendtwo_none_po_kernel(
         def load_scale_rows(source, name):
             tile = sb.tile([P, source.shape[2]], U8, name=name, align_bytes=64)
             nc.vector.memset(tile[:].bitcast(I32), 0)
-            for e in range(2):
-                nc.sync.dma_start(tile[e:P:16, :].bitcast(I32), source[0, e:16:2, :].bitcast(I32))
+            nc.sync.dma_start(tile[0:P:8, :].bitcast(I32), source[0].bitcast(I32))
             return tile
 
         def load_words(source, name):
@@ -55,10 +56,10 @@ def tile_picked_hpqhhaarhsendtwo_none_po_kernel(
                     out[:, i * n : (i + 1) * n], table[:].indirect(offsets[:, i * n // 16 : (i + 1) * n // 16])
                 )
 
-        def deal_words(out, picked):
+        def deal_words(out, picked, slots):
             nc.vector.tensor_copy(
-                out.rearrange("p (t c i) -> p c t i", t=PACK, i=4),
-                picked.rearrange("p (c i t) -> p c t i", t=PACK, i=4),
+                out.rearrange("p (t c i) -> p c t i", t=PACK, i=4)[:, :, slots, :],
+                picked.rearrange("p (c i t) -> p c t i", t=PACK, i=4)[:, :, slots, :],
             )
 
         def deal_bytes(out, picked):
@@ -67,41 +68,38 @@ def tile_picked_hpqhhaarhsendtwo_none_po_kernel(
             )
 
         def lift_odd_runs(plane):
-            for e in range(2):
-                nc.sync.dma_start(plane[2 + e : P : 32, :].bitcast(I32), plane[16 + e : P : 32, :].bitcast(I32))
+            for j in range(1, 4):
+                nc.sync.dma_start(plane[j:P:32, :].bitcast(I32), plane[8 * j : P : 32, :].bitcast(I32))
 
         k1_t = load_list(k1, "k1_t")
         d_bytes = load_scale_rows(d_scales, "d_bytes")
         offs_t = load_list(offs, "offs_t")
         x_bytes = load_scale_rows(x_scales, "x_bytes")
         n1_t = load_list(n1, "n1_t")
+        n2_t = load_list(n2, "n2_t")
         d_table = load_words(d_words, "d_table")
         x_table = load_words(x_words, "x_table")
-        n2_t = load_list(n2, "n2_t")
         cand_t = load_list(cand, "cand_t")
         n3_t = load_list(n3, "n3_t")
         n4_t = load_list(n4, "n4_t")
         n5_t = load_list(n5, "n5_t")
-        gs_t = sb.tile([P, PACK], F32, name="gs_t")
-        nc.gpsimd.dma_start(gs_t[:], gs.rearrange("(p t) o -> p (t o)", t=PACK))
-        gain = sb.tile([P, PACK], F32, name="gain")
-        nc.scalar.activation(gain[:], gs_t[:], COPY, scale=SIXTEENTH)
 
-        dk_bytes = sb.tile([P, H], U8, name="dk_bytes", tag="bytes_a", align_bytes=64)
+        dk_bytes = sb.tile([P, H], U8, name="dk_bytes", align_bytes=64)
         xq_bytes = sb.tile([P, S], U8, name="xq_bytes", align_bytes=64)
-        plane1 = sb.tile([P, H + S], U8, name="plane1", tag="bytes_b", align_bytes=64)
+        plane1 = sb.tile([P, H + S], U8, name="plane1", align_bytes=64)
         pick(dk_bytes, d_bytes, k1_t, 1)
         pick(xq_bytes, x_bytes, offs_t, 1)
         deal_bytes(plane1[:, :H], dk_bytes[:])
         nc.vector.tensor_copy(plane1[:, H:].bitcast(I32), xq_bytes[:].bitcast(I32))
         lift_odd_runs(plane1)
 
-        dk_words = sb.tile([P, H], U32, name="dk_words", tag="words_a", align_bytes=64)
-        dk_dealt = sb.tile([P, H], U32, name="dk_dealt", tag="words_b", align_bytes=64)
-        xq_words = sb.tile([P, S], U32, name="xq_words", align_bytes=64)
+        dk_words = sb.tile([P, H], U32, name="dk_words", align_bytes=64)
+        dk_dealt = sb.tile([P, H], U32, name="dk_dealt", align_bytes=64)
+        xq_words = sb.tile([P, S], U32, name="xq_words", tag="words_c", align_bytes=64)
         pick(dk_words, d_table, k1_t, 1)
-        deal_words(dk_dealt[:], dk_words[:])
+        deal_words(dk_dealt[:], dk_words[:], slice(0, 1))
         pick(xq_words, x_table, offs_t, 1)
+        deal_words(dk_dealt[:], dk_words[:], slice(1, PACK))
 
         h = []
         for t in range(PACK):
@@ -117,122 +115,125 @@ def tile_picked_hpqhhaarhsendtwo_none_po_kernel(
                 stop=True,
             )
             h_t = sb.tile([P, S], F32, name=f"h{t}")
-            nc.vector.tensor_copy(h_t[:], acc[:])
+            nc.vector.tensor_scalar(h_t[:], acc[:], SIXTEENTH, None, ALU.mult)
             h.append(h_t)
 
-        pair = [sb.tile([P, S], F32, name=f"pair{t}") for t in range(PACK)]
-        mixed = [sb.tile([P, S], F32, name=f"mixed{t}", tag=f"mixed{t}") for t in range(PACK)]
+        gain = sb.tile([P, PACK], F32, name="gain", tag="words_c", align_bytes=64)
+        nc.sync.dma_start(gain[:], gs.rearrange("(p t) o -> p (t o)", t=PACK))
+
+        pair = [sb.tile([P, 2, S], F32, name=f"pair{u}", tag=f"pair{u}", align_bytes=64) for u in range(2)]
+        mixed = [[sb.tile([P, 2, W], F32, name=f"mixed{u}{side}", tag=f"mixed{u}{side}") for side in range(2)] for u in range(2)]
         dt = [sb.tile([P, S], F32, name=f"dt{t}") for t in range(PACK)]
-        other_a = sb.tile([P, PACK, HALF], F32, name="other_a")
-        top = sb.tile([P, PACK, S], F32, name="top")
-        z_bf = [sb.tile([P, HALF, PACK], BF16, name=f"z_bf{c}", align_bytes=64) for c in range(2)]
-        z_words = sb.tile([P, S], U32, name="z_words", align_bytes=64)
         z_plane = sb.tile([P, S], U8, name="z_plane", align_bytes=64)
+        s = [sb.tile([P, S], F32, name=f"s{t}") for t in range(PACK)]
+        ds2 = [sb.tile([P, S], F32, name=f"ds2_{t}") for t in range(PACK)]
+        ds3 = [sb.tile([P, S], F32, name=f"ds3_{t}") for t in range(PACK)]
+        early, late = slice(0, EARLY), slice(EARLY, S)
 
-        def fetch_pair(t, side):
-            offsets = (n1_t, n2_t)[side]
-            nc.scalar.activation(pair[t][:, side * W : (side + 1) * W], h[t][:].indirect(offsets[:]), COPY)
-
-        def mix(t):
-            pa, pb = pair[t][:, :W], pair[t][:, W:]
-            nc.vector.tensor_tensor(mixed[t][:, :W], pa, pb, ALU.add)
-            nc.vector.tensor_tensor(mixed[t][:, W:], pa, pb, ALU.subtract)
+        def entries(offsets, cols):
+            return offsets[:, cols.start // 16 : cols.stop // 16]
 
         def put_pair(t, side):
-            offsets = (n1_t, n2_t)[side]
-            nc.scalar.activation(dt[t][:].indirect(offsets[:]), mixed[t][:, side * W : (side + 1) * W], COPY)
+            nc.scalar.activation(dt[t][:].indirect((n1_t, n2_t)[side][:]), mixed[t // 2][side][:, t % 2, :], COPY)
 
-        def fetch_other(t, c, other):
-            offsets = n3_t[:, c * HALF // 16 : (c + 1) * HALF // 16]
-            nc.scalar.activation(other[:, t, :], dt[t][:].indirect(offsets), COPY)
+        def make_z(t, cols, other, top, z_bf):
+            nc.scalar.activation(other[:, t, :], dt[t][:].indirect(entries(n3_t, cols)), COPY)
+            nc.vector.tensor_tensor(top, dt[t][:, cols], other[:, t, :], ALU.max)
+            nc.vector.tensor_scalar(z_bf[:, :, t], top, gain[:, t : t + 1], None, ALU.mult)
 
-        def weigh(t, c, other):
-            cols = slice(c * HALF, (c + 1) * HALF)
-            nc.vector.tensor_tensor(top[:, t, cols], dt[t][:, cols], other[:, t, :], ALU.max)
-            nc.vector.tensor_scalar(z_bf[c][:, :, t], top[:, t, cols], gain[:, t : t + 1], None, ALU.mult)
-
-        def quantise_z(c):
-            cols = slice(c * HALF, (c + 1) * HALF)
+        def quantise_z(z_bf, z_words, first, cols):
             nc.vector.quantize_mx(
-                out=z_words[:, cols].bitcast(FP8X4),
+                out=z_words[:, cols.start - first : cols.stop - first].bitcast(FP8X4),
                 scales=z_plane[:, cols],
-                in_=z_bf[c][:].rearrange("p w j -> p (w j)"),
+                in_=z_bf[:, cols.start - first : cols.stop - first, :].rearrange("p w j -> p (w j)"),
             )
 
-        for t in range(2):
-            fetch_pair(t, 0)
-            fetch_pair(t, 1)
-            mix(t)
-        for t in range(PACK):
-            for side in range(2):
-                put_pair(t, side)
-                if t + 2 < PACK:
-                    fetch_pair(t + 2, side)
-                else:
-                    step = 2 * (t + 2 - PACK) + side
-                    fetch_other(step, 0, other_a)
-                    weigh(step, 0, other_a)
-            if t + 2 < PACK:
-                mix(t + 2)
+        def score(t, z_words, parts):
+            rows = slice(t * P, (t + 1) * P)
+            first, last = parts[0].start, parts[-1].stop
+            acc = psum.tile([P, last - first], F32, name="acc", tag="acc")
+            for cols in parts:
+                nc.tensor.matmul_mx(
+                    out=acc[:, cols.start - first : cols.stop - first],
+                    lhsT=xc_dealt[:, rows].bitcast(FP8X4),
+                    lhsT_scale=plane2[:, rows],
+                    rhs=z_words[:, cols.start - first : cols.stop - first].bitcast(FP8X4),
+                    rhs_scale=z_plane[:, cols],
+                    start=True,
+                    stop=True,
+                )
+            nc.vector.tensor_scalar(s[t][:, first:last], acc[:], SIXTEENTH, None, ALU.mult)
 
-        xc_bytes = sb.tile([P, C], U8, name="xc_bytes", tag="bytes_b", align_bytes=64)
-        plane2 = sb.tile([P, C], U8, name="plane2", tag="bytes_a", align_bytes=64)
-        xc_words = sb.tile([P, C], U32, name="xc_words", tag="words_b", align_bytes=64)
-        xc_dealt = sb.tile([P, C], U32, name="xc_dealt", tag="words_a", align_bytes=64)
+        def send(t, cols):
+            for window, offsets in ((ds2[t], n4_t), (ds3[t], n5_t)):
+                nc.scalar.activation(window[:].indirect(entries(offsets, cols)), s[t][:, cols], COPY)
+
+        for u in range(2):
+            for t in (2 * u, 2 * u + 1):
+                for side in range(2):
+                    offsets = (n1_t, n2_t)[side]
+                    nc.scalar.activation(
+                        pair[u][:, t % 2, side * W : (side + 1) * W], h[t][:].indirect(offsets[:]), COPY
+                    )
+            for side in range(2):
+                op = (ALU.add, ALU.subtract)[side]
+                nc.vector.tensor_tensor(mixed[u][side][:], pair[u][:, :, :W], pair[u][:, :, W:], op)
+
+        xc_bytes = sb.tile([P, C], U8, name="xc_bytes", tag="pair0", align_bytes=64)
+        plane2 = sb.tile([P, C], U8, name="plane2", align_bytes=64)
+        xc_words = sb.tile([P, C], U32, name="xc_words", tag="pair1", align_bytes=64)
+        xc_dealt = sb.tile([P, C], U32, name="xc_dealt", align_bytes=64)
         pick(xc_bytes, x_bytes, cand_t, 2)
         deal_bytes(plane2[:], xc_bytes[:])
         lift_odd_runs(plane2)
         pick(xc_words, x_table, cand_t, 2)
-        deal_words(xc_dealt[:], xc_words[:])
+        deal_words(xc_dealt[:], xc_words[:], slice(0, PACK))
 
-        s = [sb.tile([P, S], F32, name=f"s{t}") for t in range(PACK)]
-
-        def score(t, cols):
-            rows = slice(t * P, (t + 1) * P)
-            acc = psum.tile([P, cols.stop - cols.start], F32, name="acc", tag="acc")
-            nc.tensor.matmul_mx(
-                out=acc[:],
-                lhsT=xc_dealt[:, rows].bitcast(FP8X4),
-                lhsT_scale=plane2[:, rows],
-                rhs=z_words[:, cols].bitcast(FP8X4),
-                rhs_scale=z_plane[:, cols],
-                start=True,
-                stop=True,
-            )
-            nc.vector.tensor_scalar(s[t][:, cols], acc[:], SIXTEENTH, None, ALU.mult)
-
-        quantise_z(0)
-        score(0, slice(0, HALF))
-
-        other_b = sb.tile([P, PACK, HALF], F32, name="other_b", tag=f"mixed{PACK - 1}")
+        other_early = sb.tile([P, PACK, EARLY], F32, name="other_early")
+        top_early = sb.tile([P, PACK, EARLY], F32, name="top_early")
+        z_early = sb.tile([P, EARLY, PACK], BF16, name="z_early", tag="z_early", align_bytes=64)
+        for side in range(2):
+            put_pair(0, side)
+            put_pair(1, side)
+        put_pair(2, 0)
+        put_pair(3, 0)
+        for t in range(2):
+            make_z(t, early, other_early, top_early[:, t, :], z_early)
+            put_pair(t + 2, 1)
+        for t in range(2, PACK):
+            make_z(t, early, other_early, top_early[:, t, :], z_early)
+        words_early = sb.tile([P, EARLY], U32, name="words_early", tag="words_early", align_bytes=64)
+        quantise_z(z_early, words_early, 0, early)
         for t in range(PACK):
-            fetch_other(t, 1, other_b)
-            weigh(t, 1, other_b)
-        quantise_z(1)
-        score(0, slice(HALF, S))
-        for t in range(1, PACK):
-            score(t, slice(0, S))
+            score(t, words_early, [early])
+
+        other_late = sb.tile([P, PACK, LATE], F32, name="other_late", tag="mixed11")
+        top_late = [
+            sb.tile([P, 2, LATE], F32, name=f"top_late{u}", tag=("z_early", "words_early")[u], align_bytes=64)
+            for u in range(2)
+        ]
+        words_late = sb.tile([P, LATE], U32, name="words_late", align_bytes=64)
+        z_late = sb.tile([P, LATE, PACK], BF16, name="z_late", align_bytes=64)
+        late_parts = [slice(EARLY, HALF), slice(HALF, S)]
+        for t in range(PACK):
+            make_z(t, late, other_late, top_late[t // 2][:, t % 2, :], z_late)
+        for t in range(PACK):
+            send(t, early)
+        for cols in late_parts:
+            quantise_z(z_late, words_late, EARLY, cols)
+        for t in range(PACK):
+            score(t, words_late, late_parts)
 
         y_bf = [sb.tile([P, HALF, PACK], BF16, name=f"y_bf{c}", align_bytes=64) for c in range(2)]
         y_words = sb.tile([P, S], U32, name="y_words", align_bytes=64)
         y_plane = sb.tile([P, S], U8, name="y_plane", align_bytes=64)
         out_rows = out_0.rearrange("(p t) c -> p t c", t=PACK)
         for t in range(PACK):
-            ds2 = sb.tile([P, 2 * S], F32, name=f"ds2_{t}")
-            ds3 = sb.tile([P, 2 * S], F32, name=f"ds3_{t}")
-            pieces = 2 if t == 0 else 1
-            n = S // pieces
-            for i in range(pieces):
-                for window, offsets in ((ds2, n4_t), (ds3, n5_t)):
-                    nc.scalar.activation(
-                        window[:].indirect(offsets[:, i * n // 16 : (i + 1) * n // 16]),
-                        s[t][:, i * n : (i + 1) * n],
-                        COPY,
-                    )
+            send(t, late)
             y = sb.tile([P, S], F32, name=f"y{t}")
             for c in range(2):
                 cols = slice(c * HALF, (c + 1) * HALF)
-                nc.vector.tensor_tensor(y[:, cols], ds2[:, cols], ds3[:, cols], ALU.max)
+                nc.vector.tensor_tensor(y[:, cols], ds2[t][:, cols], ds3[t][:, cols], ALU.max)
             nc.sync.dma_start(out_rows[:, t, :], y[:])
             for c in range(2):
                 nc.vector.tensor_copy(y_bf[c][:, :, t], y[:, c * HALF : (c + 1) * HALF])

@@ -56,67 +56,69 @@ def tile_picked_hpqhhaarhsendtwo_none_po_kernel(
                     out[:, i * n : (i + 1) * n], table[:].indirect(offsets[:, i * n // 16 : (i + 1) * n // 16])
                 )
 
-        def deal_words(out, picked, slots):
-            nc.vector.tensor_copy(
-                out.rearrange("p (t c i) -> p c t i", t=PACK, i=4)[:, :, slots, :],
-                picked.rearrange("p (c i t) -> p c t i", t=PACK, i=4)[:, :, slots, :],
-            )
+        def deal_words(out, picked, pieces):
+            n = picked.shape[1] // (16 * pieces)
+            for i in range(pieces):
+                nc.vector.tensor_copy(
+                    out.rearrange("p (t c i) -> p c t i", t=PACK, i=4)[:, i * n : (i + 1) * n],
+                    picked.rearrange("p (c i t) -> p c t i", t=PACK, i=4)[:, i * n : (i + 1) * n],
+                )
 
-        def deal_bytes(out, picked):
+        def deal_bytes(out, picked, slots):
             nc.vector.tensor_copy(
-                out.rearrange("p (t m) -> p t m", t=PACK), picked.rearrange("p (m t) -> p t m", t=PACK)
+                out.rearrange("p (t m) -> p t m", m=P), picked.rearrange("p (m t) -> p t m", t=PACK)[:, slots, :]
             )
 
         def lift_odd_runs(plane):
             for j in range(1, 4):
                 nc.sync.dma_start(plane[j:P:32, :].bitcast(I32), plane[8 * j : P : 32, :].bitcast(I32))
 
-        k1_t = load_list(k1, "k1_t")
-        d_bytes = load_scale_rows(d_scales, "d_bytes")
         offs_t = load_list(offs, "offs_t")
         x_bytes = load_scale_rows(x_scales, "x_bytes")
+        k1_t = load_list(k1, "k1_t")
+        d_bytes = load_scale_rows(d_scales, "d_bytes")
         n1_t = load_list(n1, "n1_t")
         n2_t = load_list(n2, "n2_t")
+        n3_t = load_list(n3, "n3_t")
         d_table = load_words(d_words, "d_table")
         x_table = load_words(x_words, "x_table")
         cand_t = load_list(cand, "cand_t")
-        n3_t = load_list(n3, "n3_t")
         n4_t = load_list(n4, "n4_t")
         n5_t = load_list(n5, "n5_t")
 
-        dk_bytes = sb.tile([P, H], U8, name="dk_bytes", align_bytes=64)
-        xq_bytes = sb.tile([P, S], U8, name="xq_bytes", align_bytes=64)
-        plane1 = sb.tile([P, H + S], U8, name="plane1", align_bytes=64)
-        pick(dk_bytes, d_bytes, k1_t, 1)
-        pick(xq_bytes, x_bytes, offs_t, 1)
-        deal_bytes(plane1[:, :H], dk_bytes[:])
-        nc.vector.tensor_copy(plane1[:, H:].bitcast(I32), xq_bytes[:].bitcast(I32))
+        picked_bytes = sb.tile([P, S + H], U8, name="picked_bytes", align_bytes=64)
+        plane1 = sb.tile([P, P + S + H], U8, name="plane1", align_bytes=64)
+        plane_rest = sb.tile([P, H - P], U8, name="plane_rest", align_bytes=64)
+        pick(picked_bytes[:, :S], x_bytes, offs_t, 1)
+        pick(picked_bytes[:, S:], d_bytes, k1_t, 1)
+        nc.vector.tensor_copy(plane1[:, P:].bitcast(I32), picked_bytes[:].bitcast(I32))
+        deal_bytes(plane1[:, :P], picked_bytes[:, S:], slice(0, 1))
         lift_odd_runs(plane1)
 
         dk_words = sb.tile([P, H], U32, name="dk_words", align_bytes=64)
         dk_dealt = sb.tile([P, H], U32, name="dk_dealt", align_bytes=64)
         xq_words = sb.tile([P, S], U32, name="xq_words", tag="words_c", align_bytes=64)
-        pick(dk_words, d_table, k1_t, 1)
-        deal_words(dk_dealt[:], dk_words[:], slice(0, 1))
-        pick(xq_words, x_table, offs_t, 1)
-        deal_words(dk_dealt[:], dk_words[:], slice(1, PACK))
+        pick(dk_words, d_table, k1_t, 2)
+        deal_words(dk_dealt[:], dk_words[:], 2)
+        pick(xq_words, x_table, offs_t, 2)
+        deal_bytes(plane_rest[:], plane1[:, P + S :], slice(1, PACK))
 
-        h = []
+        h = [sb.tile([P, S], F32, name=f"h{t}") for t in range(PACK)]
         for t in range(PACK):
             rows = slice(t * P, (t + 1) * P)
-            acc = psum.tile([P, S], F32, name="acc", tag="acc")
-            nc.tensor.matmul_mx(
-                out=acc[:],
-                lhsT=dk_dealt[:, rows].bitcast(FP8X4),
-                lhsT_scale=plane1[:, rows],
-                rhs=xq_words[:].bitcast(FP8X4),
-                rhs_scale=plane1[:, H:],
-                start=True,
-                stop=True,
-            )
-            h_t = sb.tile([P, S], F32, name=f"h{t}")
-            nc.vector.tensor_scalar(h_t[:], acc[:], SIXTEENTH, None, ALU.mult)
-            h.append(h_t)
+            width = HALF if t == 0 else S
+            for first in range(0, S, width):
+                acc = psum.tile([P, width], F32, name="acc", tag="acc")
+                nc.tensor.matmul_mx(
+                    out=acc[:],
+                    lhsT=dk_dealt[:, rows].bitcast(FP8X4),
+                    lhsT_scale=plane1[:, :P] if t == 0 else plane_rest[:, (t - 1) * P : t * P],
+                    rhs=xq_words[:, first : first + width].bitcast(FP8X4),
+                    rhs_scale=plane1[:, P + first : P + first + width],
+                    start=True,
+                    stop=True,
+                )
+                nc.vector.tensor_scalar(h[t][:, first : first + width], acc[:], SIXTEENTH, None, ALU.mult)
 
         gain = sb.tile([P, PACK], F32, name="gain", tag="words_c", align_bytes=64)
         nc.sync.dma_start(gain[:], gs.rearrange("(p t) o -> p (t o)", t=PACK))
@@ -184,10 +186,10 @@ def tile_picked_hpqhhaarhsendtwo_none_po_kernel(
         xc_words = sb.tile([P, C], U32, name="xc_words", tag="pair1", align_bytes=64)
         xc_dealt = sb.tile([P, C], U32, name="xc_dealt", align_bytes=64)
         pick(xc_bytes, x_bytes, cand_t, 2)
-        deal_bytes(plane2[:], xc_bytes[:])
+        deal_bytes(plane2[:], xc_bytes[:], slice(0, PACK))
         lift_odd_runs(plane2)
         pick(xc_words, x_table, cand_t, 2)
-        deal_words(xc_dealt[:], xc_words[:], slice(0, PACK))
+        deal_words(xc_dealt[:], xc_words[:], 1)
 
         other_early = sb.tile([P, PACK, EARLY], F32, name="other_early")
         top_early = sb.tile([P, PACK, EARLY], F32, name="top_early")
@@ -244,7 +246,9 @@ def tile_picked_hpqhhaarhsendtwo_none_po_kernel(
                 scales=y_plane[:, cols],
                 in_=y_bf[c][:].rearrange("p w j -> p (w j)"),
             )
-        nc.sync.dma_start(out_1[0].rearrange("p c r -> p (c r)").bitcast(I32), y_words[:].bitcast(I32))
+            nc.sync.dma_start(
+                out_1[0].rearrange("p c r -> p (c r)").bitcast(I32)[:, cols], y_words[:, cols].bitcast(I32)
+            )
         for q in range(4):
             queue = (nc.scalar, nc.sync)[q % 2]
             queue.dma_start(out_2[0, 4 * q : 4 * q + 4, :].bitcast(I32), y_plane[32 * q : 32 * q + 4, :].bitcast(I32))

@@ -246,9 +246,7 @@ def tile_picked_hpqhhaarhsendtwo_none_po_kernel(
                 scales=y_plane[:, cols],
                 in_=y_bf[c][:].rearrange("p w j -> p (w j)"),
             )
-            nc.sync.dma_start(
-                out_1[0].rearrange("p c r -> p (c r)").bitcast(I32)[:, cols], y_words[:, cols].bitcast(I32)
-            )
+        nc.sync.dma_start(out_1[0].rearrange("p c r -> p (c r)").bitcast(I32), y_words[:].bitcast(I32))
         for q in range(4):
             queue = (nc.scalar, nc.sync)[q % 2]
             queue.dma_start(out_2[0, 4 * q : 4 * q + 4, :].bitcast(I32), y_plane[32 * q : 32 * q + 4, :].bitcast(I32))

from contextlib import ExitStack

import concourse.mybir as mybir

K, T, S, G, H, W, C = 512, 1024, 256, 2048, 512, 128, 512
FLOPS = 2 * K * H * S + 2 * H * C * S

F32 = mybir.dt.float32
BF16 = mybir.dt.bfloat16
I32 = mybir.dt.int32
U32 = mybir.dt.uint32
U16 = mybir.dt.uint16
U8 = mybir.dt.uint8
FP8X4 = mybir.dt.float8_e4m3fn_x4
ALU = mybir.AluOpType
COPY = mybir.ActivationFunctionType.Copy

P = 128
PACK = 4
HALF = S // 2
EARLY = 64
LATE = S - EARLY
SIXTEENTH = 0.0625


def tile_picked_hpqhhaarhsendtwo_none_po_kernel(
    tc, x_words, x_scales, d_words, d_scales, gs, offs, k1, n1, n2, n3, cand, n4, n5, out_0, out_1, out_2
):
    nc = tc.nc

    with ExitStack() as ctx:
        lists = ctx.enter_context(tc.tile_pool(name="lists", bufs=1))
        sb = ctx.enter_context(tc.tile_pool(name="sb", bufs=1))
        psum = ctx.enter_context(tc.psum_pool(name="psum", bufs=8))

        def load_list(source, name):
            tile = lists.tile(list(source.shape), U16, name=name)
            nc.sync.dma_start(tile[:], source)
            return tile

        def load_scale_rows(source, name):
            tile = sb.tile([P, source.shape[2]], U8, name=name, align_bytes=64)
            nc.vector.memset(tile[:].bitcast(I32), 0)
            nc.sync.dma_start(tile[0:P:8, :].bitcast(I32), source[0].bitcast(I32))
            return tile

        def load_words(source, name):
            tile = sb.tile([P, source.shape[2]], U32, name=name, align_bytes=64)
            nc.sync.dma_start(tile[:].bitcast(I32), source[0].rearrange("p c r -> p (c r)").bitcast(I32))
            return tile

        def pick(out, table, offsets, pieces):
            n = out.shape[1] // pieces
            for i in range(pieces):
                nc.vector.tensor_copy(
                    out[:, i * n : (i + 1) * n], table[:].indirect(offsets[:, i * n // 16 : (i + 1) * n // 16])
                )

        def deal_words(out, picked, pieces):
            n = picked.shape[1] // (16 * pieces)
            for i in range(pieces):
                nc.vector.tensor_copy(
                    out.rearrange("p (t c i) -> p c t i", t=PACK, i=4)[:, i * n : (i + 1) * n],
                    picked.rearrange("p (c i t) -> p c t i", t=PACK, i=4)[:, i * n : (i + 1) * n],
                )

        def deal_bytes(out, picked, slots):
            nc.vector.tensor_copy(
                out.rearrange("p (t m) -> p t m", m=P), picked.rearrange("p (m t) -> p t m", t=PACK)[:, slots, :]
            )

        def lift_odd_runs(plane):
            for j in range(1, 4):
                nc.sync.dma_start(plane[j:P:32, :].bitcast(I32), plane[8 * j : P : 32, :].bitcast(I32))

        offs_t = load_list(offs, "offs_t")
        x_bytes = load_scale_rows(x_scales, "x_bytes")
        k1_t = load_list(k1, "k1_t")
        d_bytes = load_scale_rows(d_scales, "d_bytes")
        n1_t = load_list(n1, "n1_t")
        n2_t = load_list(n2, "n2_t")
        n3_t = load_list(n3, "n3_t")
        d_table = load_words(d_words, "d_table")
        x_table = load_words(x_words, "x_table")
        cand_t = load_list(cand, "cand_t")
        n4_t = load_list(n4, "n4_t")
        n5_t = load_list(n5, "n5_t")

        picked_bytes = sb.tile([P, S + H], U8, name="picked_bytes", align_bytes=64)
        plane1 = sb.tile([P, P + S + H], U8, name="plane1", align_bytes=64)
        plane_rest = sb.tile([P, H - P], U8, name="plane_rest", align_bytes=64)
        pick(picked_bytes[:, :S], x_bytes, offs_t, 1)
        pick(picked_bytes[:, S:], d_bytes, k1_t, 1)
        nc.vector.tensor_copy(plane1[:, P:].bitcast(I32), picked_bytes[:].bitcast(I32))
        deal_bytes(plane1[:, :P], picked_bytes[:, S:], slice(0, 1))
        lift_odd_runs(plane1)

        dk_words = sb.tile([P, H], U32, name="dk_words", align_bytes=64)
        dk_dealt = sb.tile([P, H], U32, name="dk_dealt", align_bytes=64)
        xq_words = sb.tile([P, S], U32, name="xq_words", tag="words_c", align_bytes=64)
        pick(dk_words, d_table, k1_t, 2)
        deal_words(dk_dealt[:], dk_words[:], 2)
        pick(xq_words, x_table, offs_t, 2)
        deal_bytes(plane_rest[:], plane1[:, P + S :], slice(1, PACK))

        h = [sb.tile([P, S], F32, name=f"h{t}") for t in range(PACK)]
        for t in range(PACK):
            rows = slice(t * P, (t + 1) * P)
            width = HALF if t == 0 else S
            for first in range(0, S, width):
                acc = psum.tile([P, width], F32, name="acc", tag="acc")
                nc.tensor.matmul_mx(
                    out=acc[:],
                    lhsT=dk_dealt[:, rows].bitcast(FP8X4),
                    lhsT_scale=plane1[:, :P] if t == 0 else plane_rest[:, (t - 1) * P : t * P],
                    rhs=xq_words[:, first : first + width].bitcast(FP8X4),
                    rhs_scale=plane1[:, P + first : P + first + width],
                    start=True,
                    stop=True,
                )
                nc.vector.tensor_scalar(h[t][:, first : first + width], acc[:], SIXTEENTH, None, ALU.mult)

        gain = sb.tile([P, PACK], F32, name="gain", tag="words_c", align_bytes=64)
        nc.sync.dma_start(gain[:], gs.rearrange("(p t) o -> p (t o)", t=PACK))

        pair = [sb.tile([P, 2, S], F32, name=f"pair{u}", tag=f"pair{u}", align_bytes=64) for u in range(2)]
        mixed = [[sb.tile([P, 2, W], F32, name=f"mixed{u}{side}", tag=f"mixed{u}{side}") for side in range(2)] for u in range(2)]
        dt = [sb.tile([P, S], F32, name=f"dt{t}") for t in range(PACK)]
        z_plane = sb.tile([P, S], U8, name="z_plane", align_bytes=64)
        s = [sb.tile([P, S], F32, name=f"s{t}") for t in range(PACK)]
        ds2 = [sb.tile([P, S], F32, name=f"ds2_{t}") for t in range(PACK)]
        ds3 = [sb.tile([P, S], F32, name=f"ds3_{t}") for t in range(PACK)]
        early, late = slice(0, EARLY), slice(EARLY, S)

        def entries(offsets, cols):
            return offsets[:, cols.start // 16 : cols.stop // 16]

        def put_pair(t, side):
            nc.scalar.activation(dt[t][:].indirect((n1_t, n2_t)[side][:]), mixed[t // 2][side][:, t % 2, :], COPY)

        def make_z(t, cols, other, top, z_bf):
            nc.scalar.activation(other[:, t, :], dt[t][:].indirect(entries(n3_t, cols)), COPY)
            nc.vector.tensor_tensor(top, dt[t][:, cols], other[:, t, :], ALU.max)
            nc.vector.tensor_scalar(z_bf[:, :, t], top, gain[:, t : t + 1], None, ALU.mult)

        def quantise_z(z_bf, z_words, first, cols):
            nc.vector.quantize_mx(
                out=z_words[:, cols.start - first : cols.stop - first].bitcast(FP8X4),
                scales=z_plane[:, cols],
                in_=z_bf[:, cols.start - first : cols.stop - first, :].rearrange("p w j -> p (w j)"),
            )

        def score(t, z_words, parts):
            rows = slice(t * P, (t + 1) * P)
            first, last = parts[0].start, parts[-1].stop
            acc = psum.tile([P, last - first], F32, name="acc", tag="acc")
            for cols in parts:
                nc.tensor.matmul_mx(
                    out=acc[:, cols.start - first : cols.stop - first],
                    lhsT=xc_dealt[:, rows].bitcast(FP8X4),
                    lhsT_scale=plane2[:, rows],
                    rhs=z_words[:, cols.start - first : cols.stop - first].bitcast(FP8X4),
                    rhs_scale=z_plane[:, cols],
                    start=True,
                    stop=True,
                )
            nc.vector.tensor_scalar(s[t][:, first:last], acc[:], SIXTEENTH, None, ALU.mult)

        def send(t, cols):
            for window, offsets in ((ds2[t], n4_t), (ds3[t], n5_t)):
                nc.scalar.activation(window[:].indirect(entries(offsets, cols)), s[t][:, cols], COPY)

        for u in range(2):
            for t in (2 * u, 2 * u + 1):
                for side in range(2):
                    offsets = (n1_t, n2_t)[side]
                    nc.scalar.activation(
                        pair[u][:, t % 2, side * W : (side + 1) * W], h[t][:].indirect(offsets[:]), COPY
                    )
            for side in range(2):
                op = (ALU.add, ALU.subtract)[side]
                nc.vector.tensor_tensor(mixed[u][side][:], pair[u][:, :, :W], pair[u][:, :, W:], op)

        xc_bytes = sb.tile([P, C], U8, name="xc_bytes", tag="pair0", align_bytes=64)
        plane2 = sb.tile([P, C], U8, name="plane2", align_bytes=64)
        xc_words = sb.tile([P, C], U32, name="xc_words", tag="pair1", align_bytes=64)
        xc_dealt = sb.tile([P, C], U32, name="xc_dealt", align_bytes=64)
        pick(xc_bytes, x_bytes, cand_t, 2)
        deal_bytes(plane2[:], xc_bytes[:], slice(0, PACK))
        lift_odd_runs(plane2)
        pick(xc_words, x_table, cand_t, 2)
        deal_words(xc_dealt[:], xc_words[:], 1)

        other_early = sb.tile([P, PACK, EARLY], F32, name="other_early")
        top_early = sb.tile([P, PACK, EARLY], F32, name="top_early")
        z_early = sb.tile([P, EARLY, PACK], BF16, name="z_early", tag="z_early", align_bytes=64)
        for side in range(2):
            put_pair(0, side)
            put_pair(1, side)
        put_pair(2, 0)
        put_pair(3, 0)
        for t in range(2):
            make_z(t, early, other_early, top_early[:, t, :], z_early)
            put_pair(t + 2, 1)
        for t in range(2, PACK):
            make_z(t, early, other_early, top_early[:, t, :], z_early)
        words_early = sb.tile([P, EARLY], U32, name="words_early", tag="words_early", align_bytes=64)
        quantise_z(z_early, words_early, 0, early)
        for t in range(PACK):
            score(t, words_early, [early])

        other_late = sb.tile([P, PACK, LATE], F32, name="other_late", tag="mixed11")
        top_late = [
            sb.tile([P, 2, LATE], F32, name=f"top_late{u}", tag=("z_early", "words_early")[u], align_bytes=64)
            for u in range(2)
        ]
        words_late = sb.tile([P, LATE], U32, name="words_late", align_bytes=64)
        z_late = sb.tile([P, LATE, PACK], BF16, name="z_late", align_bytes=64)
        late_parts = [slice(EARLY, HALF), slice(HALF, S)]
        for t in range(PACK):
            make_z(t, late, other_late, top_late[t // 2][:, t % 2, :], z_late)
        for t in range(PACK):
            send(t, early)
        for cols in late_parts:
            quantise_z(z_late, words_late, EARLY, cols)
        for t in range(PACK):
            score(t, words_late, late_parts)

        y_bf = [sb.tile([P, HALF, PACK], BF16, name=f"y_bf{c}", align_bytes=64) for c in range(2)]
        y_words = sb.tile([P, S], U32, name="y_words", align_bytes=64)
        y_plane = sb.tile([P, S], U8, name="y_plane", align_bytes=64)
        out_rows = out_0.rearrange("(p t) c -> p t c", t=PACK)
        for t in range(PACK):
            send(t, late)
            y = sb.tile([P, S], F32, name=f"y{t}")
            for c in range(2):
                cols = slice(c * HALF, (c + 1) * HALF)
                nc.vector.tensor_tensor(y[:, cols], ds2[t][:, cols], ds3[t][:, cols], ALU.max)
            nc.sync.dma_start(out_rows[:, t, :], y[:])
            for c in range(2):
                nc.vector.tensor_copy(y_bf[c][:, :, t], y[:, c * HALF : (c + 1) * HALF])
        for c in range(2):
            cols = slice(c * HALF, (c + 1) * HALF)
            nc.vector.quantize_mx(
                out=y_words[:, cols].bitcast(FP8X4),
                scales=y_plane[:, cols],
                in_=y_bf[c][:].rearrange("p w j -> p (w j)"),
            )
        nc.sync.dma_start(out_1[0].rearrange("p c r -> p (c r)").bitcast(I32), y_words[:].bitcast(I32))
        for q in range(4):
            queue = (nc.scalar, nc.sync)[q % 2]
            queue.dma_start(out_2[0, 4 * q : 4 * q + 4, :].bitcast(I32), y_plane[32 * q : 32 * q + 4, :].bitcast(I32))
